import numpy as np, ml_dtypes
CORES = [5,21,45,77,85,101,109,125,133,141,189,213]
N = 12
import mx_ref
NC, WT = 128, 2
BF = ml_dtypes.bfloat16
def setup_inputs(rng):
    def f(*shape):
        return mx_ref.flush((rng.standard_normal(shape, dtype=np.float32) * np.exp2(rng.integers(-2, 3, shape[:-1] + (1,)))).astype(BF))
    return {"w": f(N, 128, WT * 512), "x": f(N, 128, 4 * NC)}
def setup_inputs_blocks(rng):
    d = setup_inputs(rng)
    for k in ("w", "x"): d[k] = mx_ref.spread(d[k], rng, 4)
    return d
def setup_inputs_wide(rng):
    d = setup_inputs(rng)
    for k in ("w", "x"): d[k] = mx_ref.flush((d[k].astype(np.float32) * np.exp2(rng.integers(-8, 9, (N, 1, 1))).astype(np.float32)).astype(BF))
    return d
def setup_inputs_zeros(rng):
    d = setup_inputs(rng); v = d["x"].reshape(N, 128, -1, 4).copy()
    v[np.broadcast_to((rng.random((N, 1, v.shape[2], 1)) < 0.33), v.shape)] = 0
    d["x"] = v.reshape(d["x"].shape)
    return d
def reference(w, x):
    QW = [mx_ref.quantize(w[b // WT][:, 512 * (b % WT):512 * (b % WT) + 512]) for b in range(N * WT)]
    y = np.zeros((N, 128, N * WT * NC), np.float32)
    for r in range(N):
        qx = mx_ref.quantize(x[r])
        for b in range(N * WT):
            y[r][:, NC * b:NC * b + NC] = mx_ref.matmul(QW[b], qx)
    return {"y": y}

from concourse.bass import DstId, RemoteDMATransfer
from concourse.mybir import dt, ActivationFunctionType

N, WT, NC = 12, 2, 128
COLS = WT * NC
WORLD = 256
BANK, NBANKS = 512, 8

SCRATCH = {
    "wb": ("sbuf", [128, WT * 4 * NC], "bfloat16"),
    "xb": ("sbuf", [128, 4 * NC], "bfloat16"),
    "wq": ("sbuf", [128, N * COLS], "float8_e4m3fn_x4"),
    "ws": ("sbuf", [128, N * COLS], "uint8"),
    "xq": ("sbuf", [128, NC], "float8_e4m3fn_x4"),
    "xs": ("sbuf", [128, NC], "uint8"),
    "yb": ("sbuf", [128, N * COLS], "float32"),
    "ps": ("psum", [128, NBANKS * BANK], "float32"),
}
SEMAPHORES = (["ldw", "ldx", "qw", "qx", "sent", "st"]
              + ["sS%d" % j for j in range(N)] + ["sC%d" % j for j in range(N)]
              + ["mm%d" % k for k in range(N)] + ["cp%d" % k for k in range(N)])

HOP, UNIT, ONCHIP = 2.0, 1.0, 0.5

_CACHE = {}


def _bits(mask):
    return bin(mask).count("1")


def _plan(cores, topo):
    key = tuple(cores)
    if key in _CACHE:
        return _CACHE[key]
    R = list(cores)
    n = len(R)
    world = range(WORLD)

    def chip_of(c):
        return (topo.host(c), topo.chip(c))

    chips = {}
    for c in world:
        chips.setdefault(chip_of(c), []).append(c)
    mate_chip = {}
    for c in world:
        k = chip_of(c)
        if k not in mate_chip:
            mate_chip[k] = [m for m in world if topo.mates(c, m)]

    def owns_port(c):
        return topo.may_write(c, mate_chip[chip_of(c)][0])

    partner = {}
    for a in range(n):
        for b in range(n):
            if topo.mates(R[a], R[b]):
                partner[a] = b
    k0 = [r for r in range(n) if r == 0 or topo.same_plane(R[0], R[r])]
    k1 = [r for r in range(n) if r not in k0]
    d0 = [r for r in k0 if r in partner]
    L0 = d0 + [r for r in k0 if r not in partner]
    L1 = [partner[r] for r in d0] + [r for r in k1 if r not in partner]
    nd = len(d0)

    helpers = {}
    busy = set()
    for r in range(n):
        c = R[r]
        mine = [h for h in chips[chip_of(c)] if h != c]
        same = [h for h in mine if topo.die(h) == topo.die(c)]
        other = [h for h in mine if topo.die(h) != topo.die(c)]
        a0 = [h for h in same if owns_port(h)][0]
        ob = [h for h in other if not owns_port(h)] + [h for h in other if owns_port(h)]
        helpers[r] = (a0, ob[0], ob[1])
        busy.update(helpers[r])

    def relays(chip_cores, die):
        gws = [c for c in chip_cores if owns_port(c) and topo.die(c) == die]
        free = [c for c in gws if c not in busy]
        return free or gws

    jobs = {}
    relay_jobs = {}
    for L, Lo in ((L0, L1), (L1, L0)):
        m = len(L)

        def turn(i, t):
            return ((i + t) // 2) % 3

        def relay_for(i, t, die):
            o = Lo[t]
            peers = sorted((turn(k, t), k) for k in range(m)
                           if (k + t) % 2 == (i + t) % 2 and partner.get(o) != L[k])
            pos = [k for _, k in peers].index(i)
            rl = relays(mate_chip[chip_of(R[o])], die)
            return rl[pos % len(rl)]

        for i, s in enumerate(L):
            a0, a1, b1 = helpers[s]
            die_a, die_b = topo.die(R[s]), topo.die(a1)
            ra, rb = [], []
            for t, o in enumerate(Lo):
                if partner.get(o) == s:
                    continue
                near = (i + t) % 2 == 0
                rc = relay_for(i, t, die_a if near else die_b)
                finals = [R[o]] + ([R[partner[o]]] if o in partner else [])
                relay_jobs.setdefault(rc, []).append((s, finals))
                (ra if near else rb).append((turn(i, t), rc))
            ra.sort()
            rb.sort()
            da, db = [], []
            for j in range(nd, m):
                if j == i:
                    continue
                if i >= nd:
                    q = (j - i) % (m - nd)
                    (da if q <= 2 else db).append((q, R[L[j]]))
                else:
                    (da if (i + j) % 2 == 0 else db).append((j, R[L[j]]))
            da.sort()
            db.sort()
            jobs[R[s]] = ([(s, [a1, b1, a0])] + [(s, [c]) for _, c in ra[:1]] + [(s, [c]) for _, c in da])
            jobs[a0] = [(s, [c]) for _, c in ra[1:]] + ([(s, [R[partner[s]]])] if s in partner else [])
            jobs[a1] = [(s, [c]) for _, c in rb[0::2]]
            jobs[b1] = [(s, [c]) for _, c in rb[1::2]] + [(s, [c]) for _, c in db]

    avail = {}
    for j in range(n):
        avail[(R[j], j)] = 0.0

    def run(core):
        t = 0.0
        for j, dests in jobs[core]:
            local = all(chip_of(d) == chip_of(core) for d in dests)
            t = max(t, avail[(core, j)] + HOP) + (ONCHIP * len(dests) if local else UNIT)
            for d in dests:
                avail[(d, j)] = t

    for r in range(n):
        run(R[r])
    for r in range(n):
        for h in helpers[r]:
            run(h)
    for rc, jl in relay_jobs.items():
        jobs[rc] = sorted(jl, key=lambda e: avail[(rc, e[0])])
        run(rc)

    out = {}
    count = {}
    for core, jl in jobs.items():
        lst = []
        for j, dests in jl:
            on = [d for d in dests if chip_of(d) == chip_of(core)]
            off = [d for d in dests if chip_of(d) != chip_of(core)]
            groups = []
            m_off = 0
            if off:
                m_off = topo.mask(core, off[0])
                for d in off:
                    m_off &= topo.mask(core, d)
                groups.append((m_off, off))
            if on:
                m_on = topo.mask(core, on[0]) & ~m_off
                groups.append((m_on, on))
            for mask, ds in groups:
                for d in ds:
                    count[(d, j)] = _bits(mask)
            lst.append((j, groups))
        out[core] = lst
    order = [sorted(range(n), key=lambda j: avail[(R[d], j)]) for d in range(n)]
    _CACHE[key] = (out, count, order)
    return _CACHE[key]


def _send(g, T, topo, core, j, groups, codes):
    lo, hi = j * COLS, (j + 1) * COLS

    def ap():
        return T.wq[:, lo:hi].bitcast(dt.uint8) if codes else T.ws[:, lo:hi]

    sem = T.sem[("sC%d" if codes else "sS%d") % j]
    if len(groups) == 1 and len(groups[0][1]) == 1:
        mask, (d,) = groups[0]
        rid, pid = topo.addr(d, core)
        g.remote_dma(ap(), ap(), sem, T.sem.sent, pid, rid, mask)
        return _bits(mask)
    trs = []
    for mask, dests in groups:
        ids = []
        for d in dests:
            rid, pid = topo.addr(d, core)
            ids.append(DstId(rid=rid, pnc=pid))
        trs.append(RemoteDMATransfer(dst_ids=ids, dma_engine_mask=mask, remote_sem=sem,
                                     srcs=[ap()], dsts=[ap() for _ in dests]))
    g.remote_dma_fused(trs, local_sem=T.sem.sent)
    return sum(_bits(mask) for mask, _ in groups)


def rank_program(g, core, T, topo):
    jobs, count, order = _plan(T.cores, topo)
    rank = T.rank_of(core)
    mine = jobs.get(core, [])
    if rank is None and not mine:
        return
    S = T.sem

    if rank is not None:
        g.sync.dma_start(T.wb[:], T.w[:]).then_inc(S.ldw, 16)
        g.sync.dma_start(T.xb[:], T.x[:]).then_inc(S.ldx, 16)
        g.vector.wait_ge(S.ldw, 16)
        for i in range(WT):
            c0 = rank * COLS + i * NC
            g.vector.quantize_mx(T.wq[:, c0:c0 + NC], T.ws[:, c0:c0 + NC],
                                 T.wb[:, 4 * NC * i:4 * NC * (i + 1)]).then_inc(S.qw, 1)
        g.vector.wait_ge(S.ldx, 16)
        g.vector.quantize_mx(T.xq[:], T.xs[:], T.xb[:]).then_inc(S.qx, 1)

    sent = 0
    have = set()
    for j, groups in mine:
        own = rank is not None and j == rank
        if own:
            if j not in have:
                g.wait_ge(S.qw, WT)
        elif j not in have:
            g.wait_ge(S["sS%d" % j], count[(core, j)])
        sent += _send(g, T, topo, core, j, groups, False)
        if not own and j not in have:
            g.wait_ge(S["sC%d" % j], count[(core, j)])
        sent += _send(g, T, topo, core, j, groups, True)
        have.add(j)
    if sent:
        g.wait_ge(S.sent, sent)

    if rank is None:
        return

    reuse = NBANKS // WT
    for k, j in enumerate(order[rank]):
        if j == rank:
            g.tensor.wait_ge(S.qw, WT)
            g.tensor.wait_ge(S.qx, 1)
        else:
            g.tensor.wait_ge(S["sS%d" % j], count[(core, j)])
            g.tensor.wait_ge(S["sC%d" % j], count[(core, j)])
        if k >= reuse:
            g.tensor.wait_ge(S["cp%d" % (k - reuse)], WT)
        mm, cp = S["mm%d" % k], S["cp%d" % k]
        banks = [(WT * k + i) % NBANKS for i in range(WT)]
        for i in range(WT):
            c0 = j * COLS + i * NC
            g.tensor.matmul_mx(T.ps[:, BANK * banks[i]:BANK * banks[i] + NC], T.wq[:, c0:c0 + NC],
                               T.ws[:, c0:c0 + NC], T.xq[:], T.xs[:], True, True).then_inc(mm, 1)
        c0 = j * COLS
        g.vector.wait_ge(mm, WT)
        g.vector.tensor_copy(T.yb[:, c0:c0 + NC], T.ps[:, BANK * banks[0]:BANK * banks[0] + NC]).then_inc(cp, 1)
        g.scalar.wait_ge(mm, WT)
        g.scalar.activation(T.yb[:, c0 + NC:c0 + COLS], T.ps[:, BANK * banks[1]:BANK * banks[1] + NC],
                            ActivationFunctionType.Copy).then_inc(cp, 1)
        g.sync.wait_ge(cp, WT)
        g.sync.dma_start(T.y[:, c0:c0 + COLS], T.yb[:, c0:c0 + COLS]).then_inc(S.st, 16)
    g.sync.wait_ge(S.st, 16 * N)
